import numpy as np
import ml_dtypes


def mxq(x, axis, fmt="e4m3"):
    dtype, down = {"e4m3": (ml_dtypes.float8_e4m3fn, 7), "e5m2": (ml_dtypes.float8_e5m2, 14)}[fmt]
    v = np.moveaxis(np.asarray(x, np.float32).astype(ml_dtypes.bfloat16).astype(np.float64), axis, -1)
    blocks = v.reshape(v.shape[:-1] + (-1, 32))
    amax = np.abs(blocks).max(-1, keepdims=True)
    byte = np.maximum(np.where(amax > 0, np.frexp(amax)[1] - 1 + 127, 0) - down, 1)
    scale = np.exp2(byte - 127.0)
    codes = (blocks / scale).astype(np.float32).astype(dtype).astype(np.float64)
    return np.moveaxis((codes * scale).reshape(v.shape), -1, axis)


WIDE = False


def mx_kscale(k):
    if not WIDE:
        return np.ones(k)
    levels = np.array([30, -30])
    if k % 512:
        return np.exp2(np.random.permutation(np.resize(levels, k // 32))).repeat(32)
    a = np.empty((k // 512, 16))
    for p in range(k // 512):
        a[p, :8] = np.random.permutation(np.resize(levels, 8))
        for g in range(8):
            far = levels[np.abs(levels - a[p, g]) >= 10]
            a[p, g + 8] = far[np.random.randint(len(far))]
    return np.exp2(a.ravel()).repeat(32)


def f64(x):
    return np.asarray(x).astype(np.float64)


def striped(idx):
    return np.tile(np.asarray(idx).reshape(-1, 16).T, (8, 1)).astype(np.uint16)


def unstriped(offs):
    return offs[:16].T.reshape(-1).astype(np.int64)


E2M1 = np.array([0.0, 0.5, 1.0, 1.5, 2.0, 3.0, 4.0, 6.0, -0.0, -0.5, -1.0, -1.5, -2.0, -3.0, -4.0, -6.0])


def pack_weight(w, fmt):
    k, n = w.shape
    w = f64(np.asarray(w, np.float32).astype(ml_dtypes.bfloat16)).reshape(k // 32, 32, n)
    amax = np.abs(w).max(1)
    if fmt in ("e4m3", "e5m2"):
        byte = np.frexp(amax)[1] - 1 + 127 - (7 if fmt == "e4m3" else 14)
    else:
        mant, ex = np.frexp(amax / 6.0)
        byte = np.where(mant > 0.5, ex, ex - 1) + 127
    byte = np.clip(np.where(amax > 0, byte, 1), 1, 254)
    scaled = (w * np.exp2(127.0 - byte)[:, None, :]).reshape(k, n).astype(np.float32)
    by_word = np.ascontiguousarray(scaled.reshape(k // 512, 128, 4, n).transpose(0, 1, 3, 2))
    if fmt in ("e4m3", "e5m2"):
        words = by_word.astype(ml_dtypes.float8_e4m3fn if fmt == "e4m3" else ml_dtypes.float8_e5m2).view(np.uint8)
    else:
        c = by_word.astype(ml_dtypes.float4_e2m1fn).view(np.uint8) & 0xF
        words = (c[..., 0::2] | (c[..., 1::2] << 4)).reshape(k // 512, 128, 2 * n)
    return np.ascontiguousarray(words), np.ascontiguousarray(byte.astype(np.uint8).reshape(k // 512, 16, n))


def unpack_weight(words, scales, fmt):
    g, _, n = scales.shape
    words = np.ascontiguousarray(words).reshape(g, 128, n, -1)
    if fmt in ("e4m3", "e5m2"):
        vals = words.view(ml_dtypes.float8_e4m3fn if fmt == "e4m3" else ml_dtypes.float8_e5m2).astype(np.float64)
    else:
        nib = np.empty((g, 128, n, 4), np.uint8)
        nib[..., 0::2] = words & 0xF
        nib[..., 1::2] = words >> 4
        vals = E2M1[nib]
    vals = vals * np.repeat(np.exp2(scales.astype(np.float64) - 127.0), 8, axis=1)[..., None]
    return vals.transpose(0, 1, 3, 2).reshape(g * 512, n)


K, T, J, I, R, Q = 512, 512, 256, 256, 512, 1024


def setup_inputs():
    n = np.random.standard_normal
    idx = np.random.permutation(T)[:J]
    idx2 = np.random.permutation(T)[:I]
    idx3 = np.random.permutation(Q)[:I]
    fk = mx_kscale(K)
    fr = mx_kscale(R)
    xtp = pack_weight(n((K, T)) / fk[:, None], "e5m2")
    wap = pack_weight(n((K, R)) * 0.5 / np.sqrt(K) * fk[:, None] * fr, "e4m3")
    wbp = pack_weight(n((K, R)) * 1 / np.sqrt(K) * fk[:, None] / fr, "e2m1")
    return {
        "xt_words": xtp[0],
        "xt_scales": xtp[1],
        "wa_words": wap[0],
        "wa_scales": wap[1],
        "wb_words": wbp[0],
        "wb_scales": wbp[1],
        "old": (10.0 * n((J, Q))).astype(np.float32),
        "offs": striped(idx),
        "offs2": striped(idx2),
        "offs3": striped(idx3),
    }


def reference(xt_words, xt_scales, wa_words, wa_scales, wb_words, wb_scales, old, offs, offs2, offs3):
    idx = unstriped(offs)
    idx2 = unstriped(offs2)
    idx3 = unstriped(offs3)
    xtu = unpack_weight(xt_words, xt_scales, "e5m2")
    wau = unpack_weight(wa_words, wa_scales, "e4m3")
    wbu = unpack_weight(wb_words, wb_scales, "e2m1")
    xtidxg = xtu[:, idx]
    za = wau.T @ xtidxg
    ya1 = np.pad(za, ((0, 0), (1, 0)))[:, :J]
    ha = za - 0.6 * ya1
    xtidx2g = xtu[:, idx2]
    zb = wbu.T @ xtidx2g
    kb1 = np.max(zb, axis=1, keepdims=True)
    hb = np.maximum(zb - 0.4 * kb1, 0.0)
    haq = mxq(ha, 0, "e5m2")
    hbq = mxq(hb, 0, "e4m3")
    a0 = haq.T @ hbq
    pp = np.zeros((J, Q))
    pp[:, idx3] = a0
    y = 0.04 * (pp - f64(old))
    return y

@@ -1,0 +1,229 @@
+from contextlib import ExitStack
+
+import concourse.mybir as mybir
+
+K, T, J, I, R, Q = 512, 512, 256, 256, 512, 1024
+FLOPS = 2 * K * R * J + 2 * K * R * I + 2 * R * J * I
+
+F32 = mybir.dt.float32
+BF16 = mybir.dt.bfloat16
+I32 = mybir.dt.int32
+U32 = mybir.dt.uint32
+U16 = mybir.dt.uint16
+U8 = mybir.dt.uint8
+E4M3 = mybir.dt.float8_e4m3fn_x4
+E5M2 = mybir.dt.float8_e5m2_x4
+E2M1 = mybir.dt.float4_e2m1fn_x4
+ALU = mybir.AluOpType
+ACT = mybir.ActivationFunctionType
+
+P = 128
+PACK = 4
+BLOCKS = 16
+LAG = 0.6
+GATE = 0.4
+GAIN = 0.04
+SHARE = 128
+PIECES = (((0, 512), (512, 1024)), ((0, 512), (512, 768), (768, 1024)))
+
+
+def load_scale_rows(engine, plane, scales, quadrants):
+    for quadrant in quadrants:
+        engine.dma_start(
+            out=plane[32 * quadrant : 32 * quadrant + 4, :].bitcast(I32),
+            in_=scales[0, 4 * quadrant : 4 * quadrant + 4, :].bitcast(I32),
+        )
+
+
+def deal_columns(nc, dealt, raw):
+    nc.scalar.copy(
+        out=dealt.rearrange("p (t g e) -> p t g e", t=PACK, g=BLOCKS),
+        in_=raw.rearrange("p (g t e) -> p t g e", t=PACK, g=BLOCKS),
+    )
+
+
+def tile_list_meet_lagged_peakgated_placed_kernel(
+    tc, xt_words, xt_scales, wa_words, wa_scales, wb_words, wb_scales, old, offs, offs2, offs3, out
+):
+    nc = tc.nc
+    with ExitStack() as ctx:
+        lists = ctx.enter_context(tc.tile_pool(name="lists", bufs=1))
+        sb = ctx.enter_context(tc.tile_pool(name="sb", bufs=1))
+        ps = ctx.enter_context(tc.psum_pool(name="ps", bufs=1))
+
+        rows_list = lists.tile([P, J // 16], U16, name="rows_list")
+        cols_list = lists.tile([P, I // 16], U16, name="cols_list")
+        board_list = lists.tile([P, I // 16], U16, name="board_list")
+
+        x_words = sb.tile([P, T], U32, name="x_words", align_bytes=64)
+        x_plane = sb.tile([P, T], U8, name="x_plane", align_bytes=64)
+        wa_raw = sb.tile([P, R], U32, name="wa_raw", tag="wa_then_hb", align_bytes=64)
+        wb_raw = sb.tile([P, R // 2], U32, name="wb_raw", tag="wb_then_old", align_bytes=64)
+        wa_plane_raw = sb.tile([P, R], U8, name="wa_plane_raw", tag="wa_plane_then_floor", align_bytes=64)
+        wb_plane_raw = sb.tile([P, R], U8, name="wb_plane_raw", tag="wb_plane_then_old", align_bytes=64)
+        pages = [sb.tile([P, Q], F32, name="page%d" % h) for h in range(2)]
+        za_sb = sb.tile([P, (J + 1) * PACK], F32, name="za_sb", align_bytes=64)
+
+        nc.vector.memset(x_plane[:].bitcast(I32), 0)
+        nc.vector.memset(wb_plane_raw[:].bitcast(I32), 0)
+        nc.vector.memset(wa_plane_raw[:].bitcast(I32), 0)
+        nc.vector.memset(za_sb[:, 0:PACK], 0.0)
+
+        nc.gpsimd.dma_start(out=wa_raw[:].bitcast(I32), in_=wa_words[0].rearrange("p n t -> p (n t)").bitcast(I32))
+        for page in pages:
+            nc.gpsimd.memset(page[:], 0.0)
+        nc.sync.dma_start(cols_list[:], offs2)
+        nc.scalar.dma_start(out=x_words[:].bitcast(I32), in_=xt_words[0].rearrange("p n t -> p (n t)").bitcast(I32))
+        nc.sync.dma_start(rows_list[:], offs)
+        nc.scalar.dma_start(out=wb_raw[:].bitcast(I32), in_=wb_words[0].bitcast(I32))
+        load_scale_rows(nc.sync, x_plane, xt_scales, [0, 1])
+        load_scale_rows(nc.scalar, x_plane, xt_scales, [2, 3])
+        load_scale_rows(nc.sync, wb_plane_raw, wb_scales, range(4))
+        load_scale_rows(nc.sync, wa_plane_raw, wa_scales, range(4))
+        nc.sync.dma_start(board_list[:], offs3)
+
+        xb_words = sb.tile([P, I], U32, name="xb_words", align_bytes=64)
+        xb_plane = sb.tile([P, I], U8, name="xb_plane", align_bytes=64)
+        xa_words = sb.tile([P, J], U32, name="xa_words", align_bytes=64)
+        xa_plane = sb.tile([P, J], U8, name="xa_plane", align_bytes=64)
+        nc.vector.tensor_copy(xb_words[:], x_words[:].indirect(cols_list[:]))
+        nc.vector.tensor_copy(xb_plane[:], x_plane[:].indirect(cols_list[:]))
+        nc.vector.tensor_copy(xa_words[:], x_words[:].indirect(rows_list[:]))
+        nc.vector.tensor_copy(xa_plane[:], x_plane[:].indirect(rows_list[:]))
+
+        wb_dealt = sb.tile([P, 2 * R], U8, name="wb_dealt", align_bytes=64)
+        wb_plane = sb.tile([P, R], U8, name="wb_plane", align_bytes=64)
+        wa_dealt = sb.tile([P, R], U32, name="wa_dealt", align_bytes=64)
+        wa_plane = sb.tile([P, R], U8, name="wa_plane", align_bytes=64)
+        deal_columns(nc, wb_dealt[:].bitcast(U32), wb_raw[:])
+        deal_columns(nc, wb_plane[:].bitcast(U32), wb_plane_raw[:].bitcast(U32))
+        deal_columns(nc, wa_dealt[:], wa_raw[:])
+        deal_columns(nc, wa_plane[:].bitcast(U32), wa_plane_raw[:].bitcast(U32))
+
+        olds = [
+            sb.tile([P, Q], F32, name="old0", tag="wb_then_old", align_bytes=64),
+            sb.tile([P, Q], F32, name="old1", tag="wb_plane_then_old", align_bytes=64),
+        ]
+        for h in range(2):
+            nc.sync.dma_start(out=olds[h][:], in_=old[P * h : P * (h + 1), :])
+
+        zb = [ps.tile([P, 2, I], F32, name="zb%d" % u) for u in range(2)]
+        for t in range(PACK):
+            nc.tensor.matmul_mx(
+                out=zb[t // 2][:, t % 2, :],
+                lhsT=wb_dealt[:, 2 * P * t : 2 * P * (t + 1)].bitcast(E2M1),
+                lhsT_scale=wb_plane[:, P * t : P * (t + 1)],
+                rhs=xb_words[:].bitcast(E5M2),
+                rhs_scale=xb_plane[:],
+                start=True,
+                stop=True,
+            )
+        za = [ps.tile([P, PACK, P], F32, name="za%d" % h) for h in range(2)]
+        for h in range(2):
+            for t in range(PACK):
+                nc.tensor.matmul_mx(
+                    out=za[h][:, t, :],
+                    lhsT=wa_dealt[:, P * t : P * (t + 1)].bitcast(E4M3),
+                    lhsT_scale=wa_plane[:, P * t : P * (t + 1)],
+                    rhs=xa_words[:, P * h : P * (h + 1)].bitcast(E5M2),
+                    rhs_scale=xa_plane[:, P * h : P * (h + 1)],
+                    start=True,
+                    stop=True,
+                )
+
+        peak = [sb.tile([P, 2], F32, name="peak%d" % u) for u in range(2)]
+        floor = sb.tile([P, PACK], F32, name="floor", tag="wa_plane_then_floor", align_bytes=64)
+        hb_planar = sb.tile([P, PACK, I], BF16, name="hb_planar", tag="wa_then_hb", align_bytes=64)
+        for u in range(2):
+            nc.vector.tensor_reduce(out=peak[u][:], in_=zb[u][:], axis=mybir.AxisListType.X, op=ALU.max)
+        half = P * PACK
+
+        def za_views(h):
+            return (
+                za_sb[:, PACK + half * h : PACK + half * (h + 1)].rearrange("p (j t) -> p j t", t=PACK),
+                za[h][:].rearrange("p t j -> p j t"),
+            )
+
+        for u in range(2):
+            nc.scalar.activation(out=floor[:, 2 * u : 2 * u + 2], in_=peak[u][:], func=ACT.Copy, scale=-GATE)
+            for tt in range(2):
+                nc.scalar.activation(
+                    out=hb_planar[:, 2 * u + tt, :],
+                    in_=zb[u][:, tt, :],
+                    func=ACT.Relu,
+                    bias=floor[:, 2 * u + tt : 2 * u + tt + 1],
+                )
+        nc.vector.tensor_copy(*za_views(0))
+        nc.scalar.copy(*za_views(1))
+
+        ha_words = [sb.tile([P, P], U32, name="ha_words%d" % h, align_bytes=64) for h in range(2)]
+        ha_plane = [sb.tile([P, P], U8, name="ha_plane%d" % h, align_bytes=64) for h in range(2)]
+        hb = sb.tile([P, I * PACK], BF16, name="hb", tag="hb_then_ha", align_bytes=64)
+        ha = [
+            sb.tile([P, half], BF16, name="ha0", align_bytes=64),
+            sb.tile([P, half], BF16, name="ha1", tag="hb_then_ha", align_bytes=64),
+        ]
+        hb_words = sb.tile([P, I], U32, name="hb_words", align_bytes=64)
+        hb_plane = sb.tile([P, I], U8, name="hb_plane", align_bytes=64)
+
+        def lag(h):
+            nc.vector.scalar_tensor_tensor(
+                out=ha[h][:],
+                in0=za_sb[:, half * h : half * (h + 1)],
+                scalar=-LAG,
+                in1=za_sb[:, PACK + half * h : PACK + half * (h + 1)],
+                op0=ALU.mult,
+                op1=ALU.add,
+            )
+
+        def quantise_ha(h):
+            nc.vector.quantize_mx(out=ha_words[h][:].bitcast(E5M2), scales=ha_plane[h][:], in_=ha[h][:])
+
+        lag(0)
+        nc.vector.tensor_copy(
+            out=hb[:].rearrange("p (i t) -> p i t", t=PACK), in_=hb_planar[:].rearrange("p t i -> p i t")
+        )
+        quantise_ha(0)
+        nc.vector.quantize_mx(out=hb_words[:].bitcast(E4M3), scales=hb_plane[:], in_=hb[:])
+        lag(1)
+        quantise_ha(1)
+
+        a0 = [ps.tile([P, I], F32, name="a0_%d" % h) for h in range(2)]
+        for h in range(2):
+            nc.tensor.matmul_mx(
+                out=a0[h][:],
+                lhsT=ha_words[h][:].bitcast(E5M2),
+                lhsT_scale=ha_plane[h][:],
+                rhs=hb_words[:].bitcast(E4M3),
+                rhs_scale=hb_plane[:],
+                start=True,
+                stop=True,
+            )
+        scores0 = sb.tile([P, I], F32, name="scores0")
+        scores1_first = sb.tile([P, SHARE], F32, name="scores1_first", tag="scores_then_result")
+        scores1_rest = sb.tile([P, I - SHARE], F32, name="scores1_rest")
+        nc.scalar.activation(out=scores0[:], in_=a0[0][:], func=ACT.Copy, scale=GAIN)
+        nc.scalar.activation(out=pages[0][:].indirect(board_list[:]), in_=scores0[:], func=ACT.Copy)
+        nc.vector.tensor_scalar(out=scores1_first[:], in0=a0[1][:, 0:SHARE], scalar1=GAIN, scalar2=None, op0=ALU.mult)
+        nc.vector.tensor_scalar(out=scores1_rest[:], in0=a0[1][:, SHARE:I], scalar1=GAIN, scalar2=None, op0=ALU.mult)
+        nc.vector.tensor_copy(pages[1][:].indirect(board_list[:, 0 : SHARE // 16]), scores1_first[:])
+        nc.scalar.activation(
+            out=pages[1][:].indirect(board_list[:, SHARE // 16 : I // 16]), in_=scores1_rest[:], func=ACT.Copy
+        )
+
+        results = [
+            sb.tile([P, Q], F32, name="result0", tag="scores_then_result"),
+            sb.tile([P, Q], F32, name="result1"),
+        ]
+        for h in range(2):
+            for lo, hi in PIECES[h]:
+                cols = slice(lo, hi)
+                nc.vector.scalar_tensor_tensor(
+                    out=results[h][:, cols],
+                    in0=olds[h][:, cols],
+                    scalar=-GAIN,
+                    in1=pages[h][:, cols],
+                    op0=ALU.mult,
+                    op1=ALU.add,
+                )
+                nc.sync.dma_start(out=out[P * h : P * (h + 1), cols], in_=results[h][:, cols])

@@ -64,22 +64,26 @@ def tile_list_meet_lagged_peakgated_placed_kernel(
         pages = [sb.tile([P, Q], F32, name="page%d" % h) for h in range(2)]
         za_sb = sb.tile([P, (J + 1) * PACK], F32, name="za_sb", align_bytes=64)
 
-        nc.vector.memset(x_plane[:].bitcast(I32), 0)
         nc.vector.memset(wb_plane_raw[:].bitcast(I32), 0)
-        nc.vector.memset(wa_plane_raw[:].bitcast(I32), 0)
+        nc.gpsimd.memset(wa_plane_raw[:].bitcast(I32), 0)
         nc.vector.memset(za_sb[:, 0:PACK], 0.0)
 
-        nc.gpsimd.dma_start(out=wa_raw[:].bitcast(I32), in_=wa_words[0].rearrange("p n t -> p (n t)").bitcast(I32))
         for page in pages:
-            nc.gpsimd.memset(page[:], 0.0)
+            nc.vector.memset(page[:], 0.0)
+
+        load_scale_rows(nc.gpsimd, wa_plane_raw, wa_scales, [3])
+        for quadrant in range(4):
+            (nc.sync, nc.scalar)[quadrant % 2].dma_start(
+                out=x_plane[32 * quadrant : 32 * quadrant + 32, :].bitcast(I32),
+                in_=xt_scales[0:1, 4 * quadrant : 4 * quadrant + 4, :].bitcast(I32).to_broadcast([8, 4, T // 4]),
+            )
         nc.sync.dma_start(cols_list[:], offs2)
         nc.scalar.dma_start(out=x_words[:].bitcast(I32), in_=xt_words[0].rearrange("p n t -> p (n t)").bitcast(I32))
         nc.sync.dma_start(rows_list[:], offs)
         nc.scalar.dma_start(out=wb_raw[:].bitcast(I32), in_=wb_words[0].bitcast(I32))
-        load_scale_rows(nc.sync, x_plane, xt_scales, [0, 1])
-        load_scale_rows(nc.scalar, x_plane, xt_scales, [2, 3])
         load_scale_rows(nc.sync, wb_plane_raw, wb_scales, range(4))
-        load_scale_rows(nc.sync, wa_plane_raw, wa_scales, range(4))
+        nc.sync.dma_start(out=wa_raw[:].bitcast(I32), in_=wa_words[0].rearrange("p n t -> p (n t)").bitcast(I32))
+        load_scale_rows(nc.sync, wa_plane_raw, wa_scales, range(3))
         nc.sync.dma_start(board_list[:], offs3)
 
         xb_words = sb.tile([P, I], U32, name="xb_words", align_bytes=64)

@@ -23,7 +23,6 @@ BLOCKS = 16
 LAG = 0.6
 GATE = 0.4
 GAIN = 0.04
-SHARE = 128
 PIECES = (((0, 512), (512, 1024)), ((0, 512), (512, 768), (768, 1024)))
 
 
@@ -90,10 +89,10 @@ def tile_list_meet_lagged_peakgated_placed_kernel(
         xb_plane = sb.tile([P, I], U8, name="xb_plane", align_bytes=64)
         xa_words = sb.tile([P, J], U32, name="xa_words", align_bytes=64)
         xa_plane = sb.tile([P, J], U8, name="xa_plane", align_bytes=64)
-        nc.vector.tensor_copy(xb_words[:], x_words[:].indirect(cols_list[:]))
         nc.vector.tensor_copy(xb_plane[:], x_plane[:].indirect(cols_list[:]))
-        nc.vector.tensor_copy(xa_words[:], x_words[:].indirect(rows_list[:]))
         nc.vector.tensor_copy(xa_plane[:], x_plane[:].indirect(rows_list[:]))
+        nc.vector.tensor_copy(xb_words[:], x_words[:].indirect(cols_list[:]))
+        nc.vector.tensor_copy(xa_words[:], x_words[:].indirect(rows_list[:]))
 
         wb_dealt = sb.tile([P, 2 * R], U8, name="wb_dealt", align_bytes=64)
         wb_plane = sb.tile([P, R], U8, name="wb_plane", align_bytes=64)
@@ -122,11 +121,10 @@ def tile_list_meet_lagged_peakgated_placed_kernel(
                 start=True,
                 stop=True,
             )
-        za = [ps.tile([P, PACK, P], F32, name="za%d" % h) for h in range(2)]
-        for h in range(2):
+        def rows_product(h, bank):
             for t in range(PACK):
                 nc.tensor.matmul_mx(
-                    out=za[h][:, t, :],
+                    out=bank[:, t, :],
                     lhsT=wa_dealt[:, P * t : P * (t + 1)].bitcast(E4M3),
                     lhsT_scale=wa_plane[:, P * t : P * (t + 1)],
                     rhs=xa_words[:, P * h : P * (h + 1)].bitcast(E5M2),
@@ -135,6 +133,11 @@ def tile_list_meet_lagged_peakgated_placed_kernel(
                     stop=True,
                 )
 
+        za0 = ps.tile([P, PACK, P], F32, name="za0")
+        rows_product(0, za0)
+        za1 = ps.tile([P, PACK, P], F32, name="za1")
+        rows_product(1, za1)
+
         peak = [sb.tile([P, 2], F32, name="peak%d" % u) for u in range(2)]
         floor = sb.tile([P, PACK], F32, name="floor", tag="wa_plane_then_floor", align_bytes=64)
         hb_planar = sb.tile([P, PACK, I], BF16, name="hb_planar", tag="wa_then_hb", align_bytes=64)
@@ -142,10 +145,10 @@ def tile_list_meet_lagged_peakgated_placed_kernel(
             nc.vector.tensor_reduce(out=peak[u][:], in_=zb[u][:], axis=mybir.AxisListType.X, op=ALU.max)
         half = P * PACK
 
-        def za_views(h):
+        def za_views(h, bank):
             return (
                 za_sb[:, PACK + half * h : PACK + half * (h + 1)].rearrange("p (j t) -> p j t", t=PACK),
-                za[h][:].rearrange("p t j -> p j t"),
+                bank[:].rearrange("p t j -> p j t"),
             )
 
         for u in range(2):
@@ -157,63 +160,86 @@ def tile_list_meet_lagged_peakgated_placed_kernel(
                     func=ACT.Relu,
                     bias=floor[:, 2 * u + tt : 2 * u + tt + 1],
                 )
-        nc.vector.tensor_copy(*za_views(0))
-        nc.scalar.copy(*za_views(1))
+        nc.vector.tensor_copy(*za_views(0, za0))
 
         ha_words = [sb.tile([P, P], U32, name="ha_words%d" % h, align_bytes=64) for h in range(2)]
         ha_plane = [sb.tile([P, P], U8, name="ha_plane%d" % h, align_bytes=64) for h in range(2)]
-        hb = sb.tile([P, I * PACK], BF16, name="hb", tag="hb_then_ha", align_bytes=64)
-        ha = [
-            sb.tile([P, half], BF16, name="ha0", align_bytes=64),
-            sb.tile([P, half], BF16, name="ha1", tag="hb_then_ha", align_bytes=64),
-        ]
+        hb = sb.tile([P, I * PACK], BF16, name="hb", align_bytes=64)
         hb_words = sb.tile([P, I], U32, name="hb_words", align_bytes=64)
         hb_plane = sb.tile([P, I], U8, name="hb_plane", align_bytes=64)
 
         def lag(h):
+            ha = sb.tile([P, half], BF16, name="ha", align_bytes=64)
             nc.vector.scalar_tensor_tensor(
-                out=ha[h][:],
+                out=ha[:],
                 in0=za_sb[:, half * h : half * (h + 1)],
                 scalar=-LAG,
                 in1=za_sb[:, PACK + half * h : PACK + half * (h + 1)],
                 op0=ALU.mult,
                 op1=ALU.add,
             )
+            return ha
 
-        def quantise_ha(h):
-            nc.vector.quantize_mx(out=ha_words[h][:].bitcast(E5M2), scales=ha_plane[h][:], in_=ha[h][:])
+        def quantise_ha(h, ha):
+            nc.vector.quantize_mx(out=ha_words[h][:].bitcast(E5M2), scales=ha_plane[h][:], in_=ha[:])
 
-        lag(0)
-        nc.vector.tensor_copy(
-            out=hb[:].rearrange("p (i t) -> p i t", t=PACK), in_=hb_planar[:].rearrange("p t i -> p i t")
-        )
-        quantise_ha(0)
-        nc.vector.quantize_mx(out=hb_words[:].bitcast(E4M3), scales=hb_plane[:], in_=hb[:])
-        lag(1)
-        quantise_ha(1)
+        def quantise_hb(lo, hi):
+            nc.vector.quantize_mx(
+                out=hb_words[:, lo:hi].bitcast(E4M3), scales=hb_plane[:, lo:hi], in_=hb[:, PACK * lo : PACK * hi]
+            )
 
-        a0 = [ps.tile([P, I], F32, name="a0_%d" % h) for h in range(2)]
-        for h in range(2):
+        def weave_views(lo, hi):
+            return (
+                hb[:, PACK * lo : PACK * hi].rearrange("p (i t) -> p i t", t=PACK),
+                hb_planar[:, :, lo:hi].rearrange("p t i -> p i t"),
+            )
+
+        nc.scalar.copy(*za_views(1, za1))
+        nc.scalar.copy(*weave_views(P, I))
+        ha_top = lag(0)
+        nc.vector.tensor_copy(*weave_views(0, P))
+        quantise_ha(0, ha_top)
+        quantise_hb(0, P)
+        ha_low = lag(1)
+        quantise_hb(P, I)
+        quantise_ha(1, ha_low)
+
+        def scores_product(h, lo, hi):
+            bank = ps.tile([P, hi - lo], F32, name="a0_%d_%d" % (h, lo))
             nc.tensor.matmul_mx(
-                out=a0[h][:],
+                out=bank[:],
                 lhsT=ha_words[h][:].bitcast(E5M2),
                 lhsT_scale=ha_plane[h][:],
-                rhs=hb_words[:].bitcast(E4M3),
-                rhs_scale=hb_plane[:],
+                rhs=hb_words[:, lo:hi].bitcast(E4M3),
+                rhs_scale=hb_plane[:, lo:hi],
                 start=True,
                 stop=True,
             )
-        scores0 = sb.tile([P, I], F32, name="scores0")
-        scores1_first = sb.tile([P, SHARE], F32, name="scores1_first", tag="scores_then_result")
-        scores1_rest = sb.tile([P, I - SHARE], F32, name="scores1_rest")
-        nc.scalar.activation(out=scores0[:], in_=a0[0][:], func=ACT.Copy, scale=GAIN)
-        nc.scalar.activation(out=pages[0][:].indirect(board_list[:]), in_=scores0[:], func=ACT.Copy)
-        nc.vector.tensor_scalar(out=scores1_first[:], in0=a0[1][:, 0:SHARE], scalar1=GAIN, scalar2=None, op0=ALU.mult)
-        nc.vector.tensor_scalar(out=scores1_rest[:], in0=a0[1][:, SHARE:I], scalar1=GAIN, scalar2=None, op0=ALU.mult)
-        nc.vector.tensor_copy(pages[1][:].indirect(board_list[:, 0 : SHARE // 16]), scores1_first[:])
-        nc.scalar.activation(
-            out=pages[1][:].indirect(board_list[:, SHARE // 16 : I // 16]), in_=scores1_rest[:], func=ACT.Copy
-        )
+            return bank
+
+        def place(h, lo, hi, scores):
+            nc.scalar.activation(
+                out=pages[h][:].indirect(board_list[:, lo // 16 : hi // 16]), in_=scores[:], func=ACT.Copy
+            )
+
+        def scaled_on_vector(bank, scores):
+            nc.vector.tensor_scalar(out=scores[:], in0=bank[:], scalar1=GAIN, scalar2=None, op0=ALU.mult)
+
+        def scaled_on_scalar(bank, scores):
+            nc.scalar.activation(out=scores[:], in_=bank[:], func=ACT.Copy, scale=GAIN)
+
+        top_early = sb.tile([P, P], F32, name="top_early")
+        top_late = sb.tile([P, P], F32, name="top_late")
+        low_early = sb.tile([P, P], F32, name="low_early", tag="scores_then_result")
+        low_late = sb.tile([P, P], F32, name="low_late")
+        scaled_on_scalar(scores_product(0, 0, P), top_early)
+        place(0, 0, P, top_early)
+        scaled_on_vector(scores_product(0, P, I), top_late)
+        place(0, P, I, top_late)
+        scaled_on_vector(scores_product(1, 0, P), low_early)
+        scaled_on_vector(scores_product(1, P, I), low_late)
+        nc.vector.tensor_copy(pages[1][:].indirect(board_list[:, 0 : P // 16]), low_early[:])
+        place(1, P, I, low_late)
 
         results = [
             sb.tile([P, Q], F32, name="result0", tag="scores_then_result"),

from contextlib import ExitStack

import concourse.mybir as mybir

K, T, J, I, R, Q = 512, 512, 256, 256, 512, 1024
FLOPS = 2 * K * R * J + 2 * K * R * I + 2 * R * J * I

F32 = mybir.dt.float32
BF16 = mybir.dt.bfloat16
I32 = mybir.dt.int32
U32 = mybir.dt.uint32
U16 = mybir.dt.uint16
U8 = mybir.dt.uint8
E4M3 = mybir.dt.float8_e4m3fn_x4
E5M2 = mybir.dt.float8_e5m2_x4
E2M1 = mybir.dt.float4_e2m1fn_x4
ALU = mybir.AluOpType
ACT = mybir.ActivationFunctionType

P = 128
PACK = 4
BLOCKS = 16
LAG = 0.6
GATE = 0.4
GAIN = 0.04
PIECES = (((0, 512), (512, 1024)), ((0, 512), (512, 768), (768, 1024)))


def load_scale_rows(engine, plane, scales, quadrants):
    for quadrant in quadrants:
        engine.dma_start(
            out=plane[32 * quadrant : 32 * quadrant + 4, :].bitcast(I32),
            in_=scales[0, 4 * quadrant : 4 * quadrant + 4, :].bitcast(I32),
        )


def deal_columns(nc, dealt, raw):
    nc.scalar.copy(
        out=dealt.rearrange("p (t g e) -> p t g e", t=PACK, g=BLOCKS),
        in_=raw.rearrange("p (g t e) -> p t g e", t=PACK, g=BLOCKS),
    )


def tile_list_meet_lagged_peakgated_placed_kernel(
    tc, xt_words, xt_scales, wa_words, wa_scales, wb_words, wb_scales, old, offs, offs2, offs3, out
):
    nc = tc.nc
    with ExitStack() as ctx:
        lists = ctx.enter_context(tc.tile_pool(name="lists", bufs=1))
        sb = ctx.enter_context(tc.tile_pool(name="sb", bufs=1))
        ps = ctx.enter_context(tc.psum_pool(name="ps", bufs=1))

        rows_list = lists.tile([P, J // 16], U16, name="rows_list")
        cols_list = lists.tile([P, I // 16], U16, name="cols_list")
        board_list = lists.tile([P, I // 16], U16, name="board_list")

        x_words = sb.tile([P, T], U32, name="x_words", align_bytes=64)
        x_plane = sb.tile([P, T], U8, name="x_plane", align_bytes=64)
        wa_raw = sb.tile([P, R], U32, name="wa_raw", tag="wa_then_hb", align_bytes=64)
        wb_raw = sb.tile([P, R // 2], U32, name="wb_raw", tag="wb_then_old", align_bytes=64)
        wa_plane_raw = sb.tile([P, R], U8, name="wa_plane_raw", tag="wa_plane_then_floor", align_bytes=64)
        wb_plane_raw = sb.tile([P, R], U8, name="wb_plane_raw", tag="wb_plane_then_old", align_bytes=64)
        pages = [sb.tile([P, Q], F32, name="page%d" % h) for h in range(2)]
        za_sb = sb.tile([P, (J + 1) * PACK], F32, name="za_sb", align_bytes=64)

        nc.vector.memset(wb_plane_raw[:].bitcast(I32), 0)
        nc.gpsimd.memset(wa_plane_raw[:].bitcast(I32), 0)
        nc.vector.memset(za_sb[:, 0:PACK], 0.0)

        for page in pages:
            nc.vector.memset(page[:], 0.0)

        load_scale_rows(nc.gpsimd, wa_plane_raw, wa_scales, [3])
        for quadrant in range(4):
            (nc.sync, nc.scalar)[quadrant % 2].dma_start(
                out=x_plane[32 * quadrant : 32 * quadrant + 32, :].bitcast(I32),
                in_=xt_scales[0:1, 4 * quadrant : 4 * quadrant + 4, :].bitcast(I32).to_broadcast([8, 4, T // 4]),
            )
        nc.sync.dma_start(cols_list[:], offs2)
        nc.scalar.dma_start(out=x_words[:].bitcast(I32), in_=xt_words[0].rearrange("p n t -> p (n t)").bitcast(I32))
        nc.sync.dma_start(rows_list[:], offs)
        nc.scalar.dma_start(out=wb_raw[:].bitcast(I32), in_=wb_words[0].bitcast(I32))
        load_scale_rows(nc.sync, wb_plane_raw, wb_scales, range(4))
        nc.sync.dma_start(out=wa_raw[:].bitcast(I32), in_=wa_words[0].rearrange("p n t -> p (n t)").bitcast(I32))
        load_scale_rows(nc.sync, wa_plane_raw, wa_scales, range(3))
        nc.sync.dma_start(board_list[:], offs3)

        xb_words = sb.tile([P, I], U32, name="xb_words", align_bytes=64)
        xb_plane = sb.tile([P, I], U8, name="xb_plane", align_bytes=64)
        xa_words = sb.tile([P, J], U32, name="xa_words", align_bytes=64)
        xa_plane = sb.tile([P, J], U8, name="xa_plane", align_bytes=64)
        nc.vector.tensor_copy(xb_plane[:], x_plane[:].indirect(cols_list[:]))
        nc.vector.tensor_copy(xa_plane[:], x_plane[:].indirect(rows_list[:]))
        nc.vector.tensor_copy(xb_words[:], x_words[:].indirect(cols_list[:]))
        nc.vector.tensor_copy(xa_words[:], x_words[:].indirect(rows_list[:]))

        wb_dealt = sb.tile([P, 2 * R], U8, name="wb_dealt", align_bytes=64)
        wb_plane = sb.tile([P, R], U8, name="wb_plane", align_bytes=64)
        wa_dealt = sb.tile([P, R], U32, name="wa_dealt", align_bytes=64)
        wa_plane = sb.tile([P, R], U8, name="wa_plane", align_bytes=64)
        deal_columns(nc, wb_dealt[:].bitcast(U32), wb_raw[:])
        deal_columns(nc, wb_plane[:].bitcast(U32), wb_plane_raw[:].bitcast(U32))
        deal_columns(nc, wa_dealt[:], wa_raw[:])
        deal_columns(nc, wa_plane[:].bitcast(U32), wa_plane_raw[:].bitcast(U32))

        olds = [
            sb.tile([P, Q], F32, name="old0", tag="wb_then_old", align_bytes=64),
            sb.tile([P, Q], F32, name="old1", tag="wb_plane_then_old", align_bytes=64),
        ]
        for h in range(2):
            nc.sync.dma_start(out=olds[h][:], in_=old[P * h : P * (h + 1), :])

        zb = [ps.tile([P, 2, I], F32, name="zb%d" % u) for u in range(2)]
        for t in range(PACK):
            nc.tensor.matmul_mx(
                out=zb[t // 2][:, t % 2, :],
                lhsT=wb_dealt[:, 2 * P * t : 2 * P * (t + 1)].bitcast(E2M1),
                lhsT_scale=wb_plane[:, P * t : P * (t + 1)],
                rhs=xb_words[:].bitcast(E5M2),
                rhs_scale=xb_plane[:],
                start=True,
                stop=True,
            )
        def rows_product(h, bank):
            for t in range(PACK):
                nc.tensor.matmul_mx(
                    out=bank[:, t, :],
                    lhsT=wa_dealt[:, P * t : P * (t + 1)].bitcast(E4M3),
                    lhsT_scale=wa_plane[:, P * t : P * (t + 1)],
                    rhs=xa_words[:, P * h : P * (h + 1)].bitcast(E5M2),
                    rhs_scale=xa_plane[:, P * h : P * (h + 1)],
                    start=True,
                    stop=True,
                )

        za0 = ps.tile([P, PACK, P], F32, name="za0")
        rows_product(0, za0)
        za1 = ps.tile([P, PACK, P], F32, name="za1")
        rows_product(1, za1)

        peak = [sb.tile([P, 2], F32, name="peak%d" % u) for u in range(2)]
        floor = sb.tile([P, PACK], F32, name="floor", tag="wa_plane_then_floor", align_bytes=64)
        hb_planar = sb.tile([P, PACK, I], BF16, name="hb_planar", tag="wa_then_hb", align_bytes=64)
        for u in range(2):
            nc.vector.tensor_reduce(out=peak[u][:], in_=zb[u][:], axis=mybir.AxisListType.X, op=ALU.max)
        half = P * PACK

        def za_views(h, bank):
            return (
                za_sb[:, PACK + half * h : PACK + half * (h + 1)].rearrange("p (j t) -> p j t", t=PACK),
                bank[:].rearrange("p t j -> p j t"),
            )

        for u in range(2):
            nc.scalar.activation(out=floor[:, 2 * u : 2 * u + 2], in_=peak[u][:], func=ACT.Copy, scale=-GATE)
            for tt in range(2):
                nc.scalar.activation(
                    out=hb_planar[:, 2 * u + tt, :],
                    in_=zb[u][:, tt, :],
                    func=ACT.Relu,
                    bias=floor[:, 2 * u + tt : 2 * u + tt + 1],
                )
        nc.vector.tensor_copy(*za_views(0, za0))

        ha_words = [sb.tile([P, P], U32, name="ha_words%d" % h, align_bytes=64) for h in range(2)]
        ha_plane = [sb.tile([P, P], U8, name="ha_plane%d" % h, align_bytes=64) for h in range(2)]
        hb = sb.tile([P, I * PACK], BF16, name="hb", align_bytes=64)
        hb_words = sb.tile([P, I], U32, name="hb_words", align_bytes=64)
        hb_plane = sb.tile([P, I], U8, name="hb_plane", align_bytes=64)

        def lag(h):
            ha = sb.tile([P, half], BF16, name="ha", align_bytes=64)
            nc.vector.scalar_tensor_tensor(
                out=ha[:],
                in0=za_sb[:, half * h : half * (h + 1)],
                scalar=-LAG,
                in1=za_sb[:, PACK + half * h : PACK + half * (h + 1)],
                op0=ALU.mult,
                op1=ALU.add,
            )
            return ha

        def quantise_ha(h, ha):
            nc.vector.quantize_mx(out=ha_words[h][:].bitcast(E5M2), scales=ha_plane[h][:], in_=ha[:])

        def quantise_hb(lo, hi):
            nc.vector.quantize_mx(
                out=hb_words[:, lo:hi].bitcast(E4M3), scales=hb_plane[:, lo:hi], in_=hb[:, PACK * lo : PACK * hi]
            )

        def weave_views(lo, hi):
            return (
                hb[:, PACK * lo : PACK * hi].rearrange("p (i t) -> p i t", t=PACK),
                hb_planar[:, :, lo:hi].rearrange("p t i -> p i t"),
            )

        nc.scalar.copy(*za_views(1, za1))
        nc.scalar.copy(*weave_views(P, I))
        ha_top = lag(0)
        nc.vector.tensor_copy(*weave_views(0, P))
        quantise_ha(0, ha_top)
        quantise_hb(0, P)
        ha_low = lag(1)
        quantise_hb(P, I)
        quantise_ha(1, ha_low)

        def scores_product(h, lo, hi):
            bank = ps.tile([P, hi - lo], F32, name="a0_%d_%d" % (h, lo))
            nc.tensor.matmul_mx(
                out=bank[:],
                lhsT=ha_words[h][:].bitcast(E5M2),
                lhsT_scale=ha_plane[h][:],
                rhs=hb_words[:, lo:hi].bitcast(E4M3),
                rhs_scale=hb_plane[:, lo:hi],
                start=True,
                stop=True,
            )
            return bank

        def place(h, lo, hi, scores):
            nc.scalar.activation(
                out=pages[h][:].indirect(board_list[:, lo // 16 : hi // 16]), in_=scores[:], func=ACT.Copy
            )

        def scaled_on_vector(bank, scores):
            nc.vector.tensor_scalar(out=scores[:], in0=bank[:], scalar1=GAIN, scalar2=None, op0=ALU.mult)

        def scaled_on_scalar(bank, scores):
            nc.scalar.activation(out=scores[:], in_=bank[:], func=ACT.Copy, scale=GAIN)

        top_early = sb.tile([P, P], F32, name="top_early")
        top_late = sb.tile([P, P], F32, name="top_late")
        low_early = sb.tile([P, P], F32, name="low_early", tag="scores_then_result")
        low_late = sb.tile([P, P], F32, name="low_late")
        scaled_on_scalar(scores_product(0, 0, P), top_early)
        place(0, 0, P, top_early)
        scaled_on_vector(scores_product(0, P, I), top_late)
        place(0, P, I, top_late)
        scaled_on_vector(scores_product(1, 0, P), low_early)
        scaled_on_vector(scores_product(1, P, I), low_late)
        nc.vector.tensor_copy(pages[1][:].indirect(board_list[:, 0 : P // 16]), low_early[:])
        place(1, P, I, low_late)

        results = [
            sb.tile([P, Q], F32, name="result0", tag="scores_then_result"),
            sb.tile([P, Q], F32, name="result1"),
        ]
        for h in range(2):
            for lo, hi in PIECES[h]:
                cols = slice(lo, hi)
                nc.vector.scalar_tensor_tensor(
                    out=results[h][:, cols],
                    in0=olds[h][:, cols],
                    scalar=-GAIN,
                    in1=pages[h][:, cols],
                    op0=ALU.mult,
                    op1=ALU.add,
                )
                nc.sync.dma_start(out=out[P * h : P * (h + 1), cols], in_=results[h][:, cols])
